import numpy as np
import ml_dtypes


def mxq(x, axis, fmt="e4m3"):
    dtype, down = {"e4m3": (ml_dtypes.float8_e4m3fn, 7), "e5m2": (ml_dtypes.float8_e5m2, 14)}[fmt]
    v = np.moveaxis(np.asarray(x, np.float32).astype(ml_dtypes.bfloat16).astype(np.float64), axis, -1)
    blocks = v.reshape(v.shape[:-1] + (-1, 32))
    amax = np.abs(blocks).max(-1, keepdims=True)
    byte = np.maximum(np.where(amax > 0, np.frexp(amax)[1] - 1 + 127, 0) - down, 1)
    scale = np.exp2(byte - 127.0)
    codes = (blocks / scale).astype(np.float32).astype(dtype).astype(np.float64)
    return np.moveaxis((codes * scale).reshape(v.shape), -1, axis)


WIDE = False


def mx_kscale(k):
    if not WIDE:
        return np.ones(k)
    levels = np.array([10, -10, 5, -5, 0])
    if k % 512:
        return np.exp2(np.random.permutation(np.resize(levels, k // 32))).repeat(32)
    a = np.empty((k // 512, 16))
    for p in range(k // 512):
        a[p, :8] = np.random.permutation(np.resize(levels, 8))
        for g in range(8):
            far = levels[np.abs(levels - a[p, g]) >= 10]
            a[p, g + 8] = far[np.random.randint(len(far))]
    return np.exp2(a.ravel()).repeat(32)


def f64(x):
    return np.asarray(x).astype(np.float64)


def striped(idx):
    return np.tile(np.asarray(idx).reshape(-1, 16).T, (8, 1)).astype(np.uint16)


def unstriped(offs):
    return offs[:16].T.reshape(-1).astype(np.int64)


E2M1 = np.array([0.0, 0.5, 1.0, 1.5, 2.0, 3.0, 4.0, 6.0, -0.0, -0.5, -1.0, -1.5, -2.0, -3.0, -4.0, -6.0])


def pack_weight(w, fmt):
    k, n = w.shape
    w = f64(np.asarray(w, np.float32).astype(ml_dtypes.bfloat16)).reshape(k // 32, 32, n)
    amax = np.abs(w).max(1)
    if fmt == "e4m3":
        byte = np.frexp(amax)[1] - 1 + 127 - 7
    else:
        mant, ex = np.frexp(amax / 6.0)
        byte = np.where(mant > 0.5, ex, ex - 1) + 127
    byte = np.clip(np.where(amax > 0, byte, 1), 1, 254)
    scaled = (w * np.exp2(127.0 - byte)[:, None, :]).reshape(k, n).astype(np.float32)
    by_word = np.ascontiguousarray(scaled.reshape(k // 512, 128, 4, n).transpose(0, 1, 3, 2))
    if fmt == "e4m3":
        words = by_word.astype(ml_dtypes.float8_e4m3fn).view(np.uint8)
    else:
        c = by_word.astype(ml_dtypes.float4_e2m1fn).view(np.uint8) & 0xF
        words = (c[..., 0::2] | (c[..., 1::2] << 4)).reshape(k // 512, 128, 2 * n)
    return np.ascontiguousarray(words), np.ascontiguousarray(byte.astype(np.uint8).reshape(k // 512, 16, n))


def unpack_weight(words, scales, fmt):
    g, _, n = scales.shape
    words = np.ascontiguousarray(words).reshape(g, 128, n, -1)
    if fmt == "e4m3":
        vals = words.view(ml_dtypes.float8_e4m3fn).astype(np.float64)
    else:
        nib = np.empty((g, 128, n, 4), np.uint8)
        nib[..., 0::2] = words & 0xF
        nib[..., 1::2] = words >> 4
        vals = E2M1[nib]
    vals = vals * np.repeat(np.exp2(scales.astype(np.float64) - 127.0), 8, axis=1)[..., None]
    return vals.transpose(0, 1, 3, 2).reshape(g * 512, n)


D, U, T, I, V, Q = 512, 512, 2048, 256, 1024, 256


def setup_inputs():
    n = np.random.standard_normal
    idx = np.random.permutation(T)[:U]
    idx2 = np.random.permutation(U)[:I]
    idx3 = np.random.permutation(V)[:I]
    fd = mx_kscale(D)
    summp = pack_weight(n((D, T)) / fd[:, None], "e2m1")
    return {
        "query": (n((D, Q)) * 0.7 / np.sqrt(D) * fd[:, None]).astype(np.float32),
        "dquery": (n((D, Q)) * 1.0 / np.sqrt(D) * fd[:, None]).astype(np.float32),
        "summ_words": summp[0],
        "summ_scales": summp[1],
        "base": (0.002 * n((Q, V))).astype(np.float32),
        "gain": (np.random.uniform(0.5, 2.0, (1, I))).astype(np.float32),
        "offs": striped(idx),
        "offs2": striped(idx2),
        "offs3": striped(idx3),
    }


def reference(query, dquery, summ_words, summ_scales, base, gain, offs, offs2, offs3):
    idx = unstriped(offs)
    idx2 = unstriped(offs2)
    idx3 = unstriped(offs3)
    summu = unpack_weight(summ_words, summ_scales, "e2m1")
    queryq = mxq(f64(query), 0, "e4m3")
    summidxg = summu[:, idx]
    a = queryq.T @ summidxg
    dqueryq = mxq(f64(dquery), 0, "e4m3")
    b = dqueryq.T @ summidxg
    p = np.exp(a - np.max(a, axis=1, keepdims=True))
    w = p / np.sum(p, axis=1, keepdims=True)
    dw = w * (b - np.sum(w * b, axis=1, keepdims=True))
    y = (dw[:, idx2] * f64(gain) + f64(base)[:, idx3]) * 512.0
    return y

@@ -1,0 +1,136 @@
+from contextlib import ExitStack
+
+import concourse.mybir as mybir
+from concourse.masks import make_identity
+
+D, U, T, I, V, Q = 512, 512, 2048, 256, 1024, 256
+P = 128
+PACK = 4
+OUT_SCALE = 512.0
+FLOPS = 2 * 2 * D * U * Q
+
+F32 = mybir.dt.float32
+BF16 = mybir.dt.bfloat16
+I32 = mybir.dt.int32
+U32 = mybir.dt.uint32
+U16 = mybir.dt.uint16
+U8 = mybir.dt.uint8
+FP8X4 = mybir.dt.float8_e4m3fn_x4
+FP4X4 = mybir.dt.float4_e2m1fn_x4
+ALU = mybir.AluOpType
+ACT = mybir.ActivationFunctionType
+AXIS = mybir.AxisListType
+
+
+def tile_attend_masstangent_kernel(tc, query, dquery, summ_words, summ_scales, base, gain, offs, offs2, offs3, out):
+    nc = tc.nc
+    tiles = Q // P
+    with ExitStack() as ctx:
+        sb = ctx.enter_context(tc.tile_pool(name="sb", bufs=1))
+        ps = ctx.enter_context(tc.psum_pool(name="ps", bufs=1))
+
+        page_list = sb.tile([P, U // 16], U16, name="page_list")
+        slot_list = sb.tile([P, I // 16], U16, name="slot_list")
+        column_list = sb.tile([P, I // 16], U16, name="column_list")
+        store_words = sb.tile([P, T], U16, name="store_words", align_bytes=64)
+        store_scales = sb.tile([P, T], U8, name="store_scales", align_bytes=64)
+        raw = [sb.tile([P, PACK, Q], F32, name="raw%d" % k) for k in range(2)]
+        table = [sb.tile([P, V], F32, name="table%d" % j) for j in range(tiles)]
+        gain_pairs = sb.tile([P, 2], F32, name="gain_pairs")
+
+        nc.vector.memset(store_scales[:].bitcast(I32), 0)
+        nc.sync.dma_start(store_words[:].bitcast(I32), summ_words[0].bitcast(I32))
+        nc.sync.dma_start(page_list[:], offs)
+        for quad in range(4):
+            nc.sync.dma_start(
+                store_scales[32 * quad : 32 * quad + 4, :].bitcast(I32),
+                summ_scales[0, 4 * quad : 4 * quad + 4, :].bitcast(I32),
+            )
+        for k, src in enumerate((query, dquery)):
+            nc.sync.dma_start(raw[k][:], src.rearrange("(p t) q -> p t q", t=PACK))
+        nc.sync.dma_start(gain_pairs[:], gain.rearrange("o (p c) -> (o p) c", c=2))
+        nc.sync.dma_start(table[0][:], base[0:P, :])
+        nc.sync.dma_start(column_list[:], offs3)
+        nc.sync.dma_start(slot_list[:], offs2)
+        nc.sync.dma_start(table[1][:], base[P : 2 * P, :])
+
+        identity = sb.tile([P, P], F32, name="identity")
+        make_identity(nc, identity[:])
+
+        page_words = sb.tile([P, U], U16, name="page_words", align_bytes=64)
+        page_scales = sb.tile([P, U], U8, name="page_scales", align_bytes=64)
+        nc.vector.tensor_copy(page_words[:], store_words[:].indirect(page_list[:]))
+        nc.vector.tensor_copy(page_scales[:], store_scales[:].indirect(page_list[:]))
+
+        def scores(k, j):
+            grouped = sb.tile([P, P, PACK], BF16, name="grouped%d%d" % (k, j), align_bytes=64)
+            codes = sb.tile([P, P], U32, name="codes%d%d" % (k, j), align_bytes=64)
+            scales = sb.tile([P, P], U8, name="scales%d%d" % (k, j), align_bytes=64)
+            bank = ps.tile([P, U], F32, name="bank%d%d" % (k, j))
+            nc.scalar.copy(
+                grouped[:].rearrange("p (c i) t -> p c t i", i=4),
+                raw[k][:, :, j * P : (j + 1) * P].rearrange("p t (c i) -> p c t i", i=4),
+            )
+            nc.vector.quantize_mx(
+                out=codes[:].bitcast(FP8X4), scales=scales[:], in_=grouped[:].rearrange("p q t -> p (q t)")
+            )
+            nc.tensor.matmul_mx(
+                out=bank[:],
+                lhsT=codes[:].bitcast(FP8X4),
+                lhsT_scale=scales[:],
+                rhs=page_words[:].bitcast(FP4X4),
+                rhs_scale=page_scales[:],
+                start=True,
+                stop=True,
+            )
+            return bank
+
+        a = [scores(0, j) for j in range(tiles)]
+        b = [scores(1, j) for j in range(tiles)]
+
+        def column(name, j):
+            return sb.tile([P, 1], F32, name="%s%d" % (name, j))
+
+        def wide(name, j, width):
+            return sb.tile([P, width], F32, name="%s%d" % (name, j))
+
+        p = [wide("p", j, U) for j in range(tiles)]
+        total = [column("total", j) for j in range(tiles)]
+        for j in range(tiles):
+            neg_max = column("neg_max", j)
+            nc.vector.tensor_reduce(neg_max[:], a[j][:], AXIS.X, ALU.max, negate=True)
+            nc.scalar.activation(p[j][:], a[j][:], ACT.Exp, bias=neg_max[:], accum_out=total[j][:])
+
+        picked = [wide("picked", j, I) for j in range(tiles)]
+        nc.vector.tensor_copy(picked[0][:], table[0][:].indirect(column_list[:]))
+
+        w = [wide("w", j, U) for j in range(tiles)]
+        mean = [column("mean", j) for j in range(tiles)]
+        for j in range(tiles):
+            inv = column("inv", j)
+            wb = wide("wb", j, U)
+            nc.vector.reciprocal(inv[:], total[j][:])
+            nc.scalar.activation(w[j][:], p[j][:], ACT.Copy, scale=inv[:])
+            nc.vector.scalar_tensor_tensor(wb[:], p[j][:], inv[:], b[j][:], ALU.mult, ALU.mult, accum_out=mean[j][:])
+
+        gain_bank = ps.tile([P, 2, P], F32, name="gain_bank")
+        for c in range(2):
+            nc.tensor.transpose(gain_bank[:, c, :], gain_pairs[:, c : c + 1].to_broadcast([P, P]), identity[:])
+        gain_rows = sb.tile([P, I], F32, name="gain_rows")
+        nc.scalar.activation(
+            gain_rows[:].rearrange("m (p c) -> m p c", c=2),
+            gain_bank[:].rearrange("m c p -> m p c"),
+            ACT.Copy,
+            scale=OUT_SCALE,
+        )
+
+        dw = [wide("dw", j, U) for j in range(tiles)]
+        for j in range(tiles):
+            nc.vector.scalar_tensor_tensor(dw[j][:], b[j][:], mean[j][:], w[j][:], ALU.subtract, ALU.mult)
+        nc.vector.tensor_copy(picked[1][:], table[1][:].indirect(column_list[:]))
+        for j in range(tiles):
+            change = wide("change", j, I)
+            result = wide("result", j, I)
+            nc.vector.tensor_tensor(change[:], dw[j][:].indirect(slot_list[:]), gain_rows[:], ALU.mult)
+            nc.vector.scalar_tensor_tensor(result[:], picked[j][:], OUT_SCALE, change[:], ALU.mult, ALU.add)
+            nc.sync.dma_start(out[j * P : (j + 1) * P, :], result[:])

@@ -48,11 +48,11 @@ def tile_attend_masstangent_kernel(tc, query, dquery, summ_words, summ_scales, b
             )
         for k, src in enumerate((query, dquery)):
             nc.sync.dma_start(raw[k][:], src.rearrange("(p t) q -> p t q", t=PACK))
-        nc.sync.dma_start(gain_pairs[:], gain.rearrange("o (p c) -> (o p) c", c=2))
-        nc.sync.dma_start(table[0][:], base[0:P, :])
         nc.sync.dma_start(column_list[:], offs3)
-        nc.sync.dma_start(slot_list[:], offs2)
+        nc.sync.dma_start(table[0][:], base[0:P, :])
+        nc.sync.dma_start(gain_pairs[:], gain.rearrange("o (p c) -> (o p) c", c=2))
         nc.sync.dma_start(table[1][:], base[P : 2 * P, :])
+        nc.sync.dma_start(slot_list[:], offs2)
 
         identity = sb.tile([P, P], F32, name="identity")
         make_identity(nc, identity[:])
@@ -63,10 +63,10 @@ def tile_attend_masstangent_kernel(tc, query, dquery, summ_words, summ_scales, b
         nc.vector.tensor_copy(page_scales[:], store_scales[:].indirect(page_list[:]))
 
         def scores(k, j):
-            grouped = sb.tile([P, P, PACK], BF16, name="grouped%d%d" % (k, j), align_bytes=64)
+            grouped = sb.tile([P, P, PACK], BF16, name="grouped%d%d" % (k, j), tag="grouped%d%d" % (k, j), align_bytes=64)
             codes = sb.tile([P, P], U32, name="codes%d%d" % (k, j), align_bytes=64)
             scales = sb.tile([P, P], U8, name="scales%d%d" % (k, j), align_bytes=64)
-            bank = ps.tile([P, U], F32, name="bank%d%d" % (k, j))
+            bank = ps.tile([P, U], F32, name="bank%d%d" % (k, j), tag="bank%d%d" % (k, j))
             nc.scalar.copy(
                 grouped[:].rearrange("p (c i) t -> p c t i", i=4),
                 raw[k][:, :, j * P : (j + 1) * P].rearrange("p t (c i) -> p c t i", i=4),
@@ -86,7 +86,7 @@ def tile_attend_masstangent_kernel(tc, query, dquery, summ_words, summ_scales, b
             return bank
 
         a = [scores(0, j) for j in range(tiles)]
-        b = [scores(1, j) for j in range(tiles)]
+        b = {}
 
         def column(name, j):
             return sb.tile([P, 1], F32, name="%s%d" % (name, j))
@@ -99,21 +99,29 @@ def tile_attend_masstangent_kernel(tc, query, dquery, summ_words, summ_scales, b
         for j in range(tiles):
             neg_max = column("neg_max", j)
             nc.vector.tensor_reduce(neg_max[:], a[j][:], AXIS.X, ALU.max, negate=True)
+            b[j] = scores(1, j)
             nc.scalar.activation(p[j][:], a[j][:], ACT.Exp, bias=neg_max[:], accum_out=total[j][:])
 
-        picked = [wide("picked", j, I) for j in range(tiles)]
-        nc.vector.tensor_copy(picked[0][:], table[0][:].indirect(column_list[:]))
+        picked, w, mean = {}, {}, {}
 
-        w = [wide("w", j, U) for j in range(tiles)]
-        mean = [column("mean", j) for j in range(tiles)]
+        def gather_columns(j, tag):
+            picked[j] = sb.tile([P, I], F32, name="picked%d" % j, tag=tag, align_bytes=64)
+            nc.vector.tensor_copy(picked[j][:], table[j][:].indirect(column_list[:]))
+
+        gather_columns(0, "grouped10")
         for j in range(tiles):
             inv = column("inv", j)
-            wb = wide("wb", j, U)
             nc.vector.reciprocal(inv[:], total[j][:])
+            w[j] = wide("w", j, U)
             nc.scalar.activation(w[j][:], p[j][:], ACT.Copy, scale=inv[:])
-            nc.vector.scalar_tensor_tensor(wb[:], p[j][:], inv[:], b[j][:], ALU.mult, ALU.mult, accum_out=mean[j][:])
+            pb = sb.tile([P, U], F32, name="pb%d" % j, tag="pb%d" % j, align_bytes=64)
+            weighted = column("weighted", j)
+            nc.vector.scalar_tensor_tensor(pb[:], b[j][:], 1.0, p[j][:], ALU.mult, ALU.mult, accum_out=weighted[:])
+            mean[j] = column("mean", j)
+            nc.scalar.activation(mean[j][:], weighted[:], ACT.Copy, scale=inv[:])
+        gather_columns(1, "pb0")
 
-        gain_bank = ps.tile([P, 2, P], F32, name="gain_bank")
+        gain_bank = ps.tile([P, 2, P], F32, name="gain_bank", tag="bank00")
         for c in range(2):
             nc.tensor.transpose(gain_bank[:, c, :], gain_pairs[:, c : c + 1].to_broadcast([P, P]), identity[:])
         gain_rows = sb.tile([P, I], F32, name="gain_rows")
@@ -125,12 +133,12 @@ def tile_attend_masstangent_kernel(tc, query, dquery, summ_words, summ_scales, b
         )
 
         dw = [wide("dw", j, U) for j in range(tiles)]
+        change = [wide("change", j, I) for j in range(tiles)]
         for j in range(tiles):
             nc.vector.scalar_tensor_tensor(dw[j][:], b[j][:], mean[j][:], w[j][:], ALU.subtract, ALU.mult)
-        nc.vector.tensor_copy(picked[1][:], table[1][:].indirect(column_list[:]))
         for j in range(tiles):
-            change = wide("change", j, I)
+            nc.vector.tensor_tensor(change[j][:], dw[j][:].indirect(slot_list[:]), gain_rows[:], ALU.mult)
+        for j in range(tiles):
             result = wide("result", j, I)
-            nc.vector.tensor_tensor(change[:], dw[j][:].indirect(slot_list[:]), gain_rows[:], ALU.mult)
-            nc.vector.scalar_tensor_tensor(result[:], picked[j][:], OUT_SCALE, change[:], ALU.mult, ALU.add)
+            nc.vector.scalar_tensor_tensor(result[:], picked[j][:], OUT_SCALE, change[j][:], ALU.mult, ALU.add)
             nc.sync.dma_start(out[j * P : (j + 1) * P, :], result[:])

from contextlib import ExitStack

import concourse.mybir as mybir
from concourse.masks import make_identity

D, U, T, I, V, Q = 512, 512, 2048, 256, 1024, 256
P = 128
PACK = 4
OUT_SCALE = 512.0
FLOPS = 2 * 2 * D * U * Q

F32 = mybir.dt.float32
BF16 = mybir.dt.bfloat16
I32 = mybir.dt.int32
U32 = mybir.dt.uint32
U16 = mybir.dt.uint16
U8 = mybir.dt.uint8
FP8X4 = mybir.dt.float8_e4m3fn_x4
FP4X4 = mybir.dt.float4_e2m1fn_x4
ALU = mybir.AluOpType
ACT = mybir.ActivationFunctionType
AXIS = mybir.AxisListType


def tile_attend_masstangent_kernel(tc, query, dquery, summ_words, summ_scales, base, gain, offs, offs2, offs3, out):
    nc = tc.nc
    tiles = Q // P
    with ExitStack() as ctx:
        sb = ctx.enter_context(tc.tile_pool(name="sb", bufs=1))
        ps = ctx.enter_context(tc.psum_pool(name="ps", bufs=1))

        page_list = sb.tile([P, U // 16], U16, name="page_list")
        slot_list = sb.tile([P, I // 16], U16, name="slot_list")
        column_list = sb.tile([P, I // 16], U16, name="column_list")
        store_words = sb.tile([P, T], U16, name="store_words", align_bytes=64)
        store_scales = sb.tile([P, T], U8, name="store_scales", align_bytes=64)
        raw = [sb.tile([P, PACK, Q], F32, name="raw%d" % k) for k in range(2)]
        table = [sb.tile([P, V], F32, name="table%d" % j) for j in range(tiles)]
        gain_pairs = sb.tile([P, 2], F32, name="gain_pairs")

        nc.vector.memset(store_scales[:].bitcast(I32), 0)
        nc.sync.dma_start(store_words[:].bitcast(I32), summ_words[0].bitcast(I32))
        nc.sync.dma_start(page_list[:], offs)
        for quad in range(4):
            nc.sync.dma_start(
                store_scales[32 * quad : 32 * quad + 4, :].bitcast(I32),
                summ_scales[0, 4 * quad : 4 * quad + 4, :].bitcast(I32),
            )
        for k, src in enumerate((query, dquery)):
            nc.sync.dma_start(raw[k][:], src.rearrange("(p t) q -> p t q", t=PACK))
        nc.sync.dma_start(column_list[:], offs3)
        nc.sync.dma_start(table[0][:], base[0:P, :])
        nc.sync.dma_start(gain_pairs[:], gain.rearrange("o (p c) -> (o p) c", c=2))
        nc.sync.dma_start(table[1][:], base[P : 2 * P, :])
        nc.sync.dma_start(slot_list[:], offs2)

        identity = sb.tile([P, P], F32, name="identity")
        make_identity(nc, identity[:])

        page_words = sb.tile([P, U], U16, name="page_words", align_bytes=64)
        page_scales = sb.tile([P, U], U8, name="page_scales", align_bytes=64)
        nc.vector.tensor_copy(page_words[:], store_words[:].indirect(page_list[:]))
        nc.vector.tensor_copy(page_scales[:], store_scales[:].indirect(page_list[:]))

        def scores(k, j):
            grouped = sb.tile([P, P, PACK], BF16, name="grouped%d%d" % (k, j), tag="grouped%d%d" % (k, j), align_bytes=64)
            codes = sb.tile([P, P], U32, name="codes%d%d" % (k, j), align_bytes=64)
            scales = sb.tile([P, P], U8, name="scales%d%d" % (k, j), align_bytes=64)
            bank = ps.tile([P, U], F32, name="bank%d%d" % (k, j), tag="bank%d%d" % (k, j))
            nc.scalar.copy(
                grouped[:].rearrange("p (c i) t -> p c t i", i=4),
                raw[k][:, :, j * P : (j + 1) * P].rearrange("p t (c i) -> p c t i", i=4),
            )
            nc.vector.quantize_mx(
                out=codes[:].bitcast(FP8X4), scales=scales[:], in_=grouped[:].rearrange("p q t -> p (q t)")
            )
            nc.tensor.matmul_mx(
                out=bank[:],
                lhsT=codes[:].bitcast(FP8X4),
                lhsT_scale=scales[:],
                rhs=page_words[:].bitcast(FP4X4),
                rhs_scale=page_scales[:],
                start=True,
                stop=True,
            )
            return bank

        a = [scores(0, j) for j in range(tiles)]
        b = {}

        def column(name, j):
            return sb.tile([P, 1], F32, name="%s%d" % (name, j))

        def wide(name, j, width):
            return sb.tile([P, width], F32, name="%s%d" % (name, j))

        p = [wide("p", j, U) for j in range(tiles)]
        total = [column("total", j) for j in range(tiles)]
        for j in range(tiles):
            neg_max = column("neg_max", j)
            nc.vector.tensor_reduce(neg_max[:], a[j][:], AXIS.X, ALU.max, negate=True)
            b[j] = scores(1, j)
            nc.scalar.activation(p[j][:], a[j][:], ACT.Exp, bias=neg_max[:], accum_out=total[j][:])

        picked, w, mean = {}, {}, {}

        def gather_columns(j, tag):
            picked[j] = sb.tile([P, I], F32, name="picked%d" % j, tag=tag, align_bytes=64)
            nc.vector.tensor_copy(picked[j][:], table[j][:].indirect(column_list[:]))

        gather_columns(0, "grouped10")
        for j in range(tiles):
            inv = column("inv", j)
            nc.vector.reciprocal(inv[:], total[j][:])
            w[j] = wide("w", j, U)
            nc.scalar.activation(w[j][:], p[j][:], ACT.Copy, scale=inv[:])
            pb = sb.tile([P, U], F32, name="pb%d" % j, tag="pb%d" % j, align_bytes=64)
            weighted = column("weighted", j)
            nc.vector.scalar_tensor_tensor(pb[:], b[j][:], 1.0, p[j][:], ALU.mult, ALU.mult, accum_out=weighted[:])
            mean[j] = column("mean", j)
            nc.scalar.activation(mean[j][:], weighted[:], ACT.Copy, scale=inv[:])
        gather_columns(1, "pb0")

        gain_bank = ps.tile([P, 2, P], F32, name="gain_bank", tag="bank00")
        for c in range(2):
            nc.tensor.transpose(gain_bank[:, c, :], gain_pairs[:, c : c + 1].to_broadcast([P, P]), identity[:])
        gain_rows = sb.tile([P, I], F32, name="gain_rows")
        nc.scalar.activation(
            gain_rows[:].rearrange("m (p c) -> m p c", c=2),
            gain_bank[:].rearrange("m c p -> m p c"),
            ACT.Copy,
            scale=OUT_SCALE,
        )

        dw = [wide("dw", j, U) for j in range(tiles)]
        change = [wide("change", j, I) for j in range(tiles)]
        for j in range(tiles):
            nc.vector.scalar_tensor_tensor(dw[j][:], b[j][:], mean[j][:], w[j][:], ALU.subtract, ALU.mult)
        for j in range(tiles):
            nc.vector.tensor_tensor(change[j][:], dw[j][:].indirect(slot_list[:]), gain_rows[:], ALU.mult)
        for j in range(tiles):
            result = wide("result", j, I)
            nc.vector.scalar_tensor_tensor(result[:], picked[j][:], OUT_SCALE, change[j][:], ALU.mult, ALU.add)
            nc.sync.dma_start(out[j * P : (j + 1) * P, :], result[:])
